import numpy as np
import ml_dtypes


def mxq(x, axis, fmt="e4m3"):
    dtype, down = {"e4m3": (ml_dtypes.float8_e4m3fn, 7), "e5m2": (ml_dtypes.float8_e5m2, 14)}[fmt]
    v = np.moveaxis(np.asarray(x, np.float32).astype(ml_dtypes.bfloat16).astype(np.float64), axis, -1)
    blocks = v.reshape(v.shape[:-1] + (-1, 32))
    amax = np.abs(blocks).max(-1, keepdims=True)
    byte = np.maximum(np.where(amax > 0, np.frexp(amax)[1] - 1 + 127, 0) - down, 1)
    scale = np.exp2(byte - 127.0)
    codes = (blocks / scale).astype(np.float32).astype(dtype).astype(np.float64)
    return np.moveaxis((codes * scale).reshape(v.shape), -1, axis)


WIDE = False


def mx_kscale(k):
    if not WIDE:
        return np.ones(k)
    levels = np.array([10, -10, 5, -5, 0])
    if k % 512:
        return np.exp2(np.random.permutation(np.resize(levels, k // 32))).repeat(32)
    a = np.empty((k // 512, 16))
    for p in range(k // 512):
        a[p, :8] = np.random.permutation(np.resize(levels, 8))
        for g in range(8):
            far = levels[np.abs(levels - a[p, g]) >= 10]
            a[p, g + 8] = far[np.random.randint(len(far))]
    return np.exp2(a.ravel()).repeat(32)


def f64(x):
    return np.asarray(x).astype(np.float64)


def striped(idx):
    return np.tile(idx.reshape(-1, 16).T, (8, 1)).astype(np.uint16)


def unstriped(offs):
    return offs[:16].T.reshape(-1).astype(np.int64)


E2M1 = np.array([0.0, 0.5, 1.0, 1.5, 2.0, 3.0, 4.0, 6.0, -0.0, -0.5, -1.0, -1.5, -2.0, -3.0, -4.0, -6.0])


def pack_weight(w, fmt):
    k, n = w.shape
    w = f64(np.asarray(w, np.float32).astype(ml_dtypes.bfloat16)).reshape(k // 32, 32, n)
    amax = np.abs(w).max(1)
    if fmt == "e4m3":
        byte = np.frexp(amax)[1] - 1 + 127 - 7
    else:
        mant, ex = np.frexp(amax / 6.0)
        byte = np.where(mant > 0.5, ex, ex - 1) + 127
    byte = np.clip(np.where(amax > 0, byte, 1), 1, 254)
    scaled = (w * np.exp2(127.0 - byte)[:, None, :]).reshape(k, n).astype(np.float32)
    by_word = np.ascontiguousarray(scaled.reshape(k // 512, 128, 4, n).transpose(0, 1, 3, 2))
    if fmt == "e4m3":
        words = by_word.astype(ml_dtypes.float8_e4m3fn).view(np.uint8)
    else:
        c = by_word.astype(ml_dtypes.float4_e2m1fn).view(np.uint8) & 0xF
        words = (c[..., 0::2] | (c[..., 1::2] << 4)).reshape(k // 512, 128, 2 * n)
    return np.ascontiguousarray(words), np.ascontiguousarray(byte.astype(np.uint8).reshape(k // 512, 16, n))


def unpack_weight(words, scales, fmt):
    g, _, n = scales.shape
    words = np.ascontiguousarray(words).reshape(g, 128, n, -1)
    if fmt == "e4m3":
        vals = words.view(ml_dtypes.float8_e4m3fn).astype(np.float64)
    else:
        nib = np.empty((g, 128, n, 4), np.uint8)
        nib[..., 0::2] = words & 0xF
        nib[..., 1::2] = words >> 4
        vals = E2M1[nib]
    vals = vals * np.repeat(np.exp2(scales.astype(np.float64) - 127.0), 8, axis=1)[..., None]
    return vals.transpose(0, 1, 3, 2).reshape(g * 512, n)


def gelu(v):
    return 0.5 * v * (1.0 + np.tanh(np.sqrt(2.0 / np.pi) * (v + 0.044715 * v**3)))


def bf(x):
    return np.asarray(x, np.float32).astype(ml_dtypes.bfloat16)


def planes(Y):
    n, m = Y.shape
    b = f64(bf(Y)).reshape(n // 32, 32, m)
    amax = np.abs(b).max(1)
    byte = np.clip(np.where(amax > 0, np.frexp(amax)[1] - 1 + 127 - 7, 1), 1, 254)
    codes = (b * np.exp2(127.0 - byte)[:, None, :]).reshape(n, m).astype(np.float32).astype(ml_dtypes.float8_e4m3fn).view(np.uint8)
    words = codes.reshape(n // 512, 128, 4, m).transpose(0, 1, 3, 2)
    return np.ascontiguousarray(words), np.ascontiguousarray(byte.astype(np.uint8).reshape(n // 512, 16, m))


K, T, S, H, T2, P, N = 1024, 2048, 1024, 512, 2048, 1024, 1024

def setup_inputs():
    n = np.random.standard_normal
    s = mx_kscale(K)[:, None]
    u = mx_kscale(H)[:, None]
    col = np.exp(0.8 * n(N))
    tab_words, tab_scales = pack_weight(n((K, T)) * s, "e4m3")
    w4_words, w4_scales = pack_weight(n((K, H)) / np.sqrt(K) / s * u.T, "e2m1")
    return {
        "tab_words": tab_words,
        "tab_scales": tab_scales,
        "offs": striped(np.random.permutation(T)[:S]),
        "offs2": striped(np.random.permutation(T2)[:S]),
        "offs3": striped(np.random.permutation(T2)[:P]),
        "w1": (n((K, H)) / np.sqrt(K) / s * u.T).astype(np.float32),
        "w4_words": w4_words,
        "w4_scales": w4_scales,
        "page0": (n((H, T2)) * u).astype(np.float32),
        "gain": np.exp(0.4 * n(H)).astype(np.float32),
        "w2": (n((H, N)) / np.sqrt(H) / u * col).astype(np.float32),
        "b2": (0.7 * n(N) * col).astype(np.float32),
    }

def reference(tab_words, tab_scales, offs, offs2, offs3, w1, w4_words, w4_scales, page0, gain, w2, b2):
    v = unpack_weight(tab_words, tab_scales, "e4m3")[:, unstriped(offs)]
    w4 = unpack_weight(w4_words, w4_scales, "e2m1")
    h1 = mxq(f64(w1), 0, "e4m3").T @ v
    h4 = w4.T @ v
    h = np.maximum(h1, h4)
    page = f64(page0).copy()
    l2 = unstriped(offs2)
    page[:, l2] = page[:, l2] + h
    x = page[:, unstriped(offs3)] * f64(gain)[:, None]
    y = (mxq(f64(w2), 0, "e4m3").T @ mxq(x, 0, "e4m3")) + f64(b2)[:, None]
    words, scales = planes(y)
    return y, words, scales

@@ -1,0 +1,282 @@
+from contextlib import ExitStack
+
+import concourse.mybir as mybir
+
+K, T, S, H, T2, PICKED, N = 1024, 2048, 1024, 512, 2048, 1024, 1024
+FLOPS = 2 * (2 * K * H * S + H * N * PICKED)
+
+F32 = mybir.dt.float32
+BF16 = mybir.dt.bfloat16
+I32 = mybir.dt.int32
+U32 = mybir.dt.uint32
+U16 = mybir.dt.uint16
+U8 = mybir.dt.uint8
+FP8X4 = mybir.dt.float8_e4m3fn_x4
+FP4X4 = mybir.dt.float4_e2m1fn_x4
+ALU = mybir.AluOpType
+ACT = mybir.ActivationFunctionType
+
+P = 128
+PACK = 4
+PASSES = K // (P * PACK)
+GROUPS = N // (P * PACK)
+BANK = 512
+CHUNK = 256
+CHUNKS = PICKED // CHUNK
+
+
+def tile_list_lift_fault_updates_kernel(
+    tc, tab_words, tab_scales, offs, offs2, offs3, w1, w4_words, w4_scales, page0, gain, w2, b2, out_0, out_1, out_2
+):
+    nc = tc.nc
+    with ExitStack() as ctx:
+        keep = ctx.enter_context(tc.tile_pool(name="keep", bufs=1))
+        big = ctx.enter_context(tc.tile_pool(name="big", bufs=4))
+        ring = ctx.enter_context(tc.tile_pool(name="ring", bufs=2))
+
+        list1 = keep.tile([P, S // 16], U16, name="list1")
+        list2 = keep.tile([P, S // 16], U16, name="list2")
+        list3 = keep.tile([P, PICKED // 16], U16, name="list3")
+
+        def slot(shape, dtype, name, tag):
+            return keep.tile(shape, dtype, name=name, tag=tag, align_bytes=64)
+
+        tab_scale_rows = slot([P, T], U8, "tab_scale_rows", "A")
+        v_scales = keep.tile([P, PASSES, S], U8, name="v_scales", align_bytes=64)
+        w4_planes = keep.tile([P, PASSES, H], U8, name="w4_planes", align_bytes=64)
+
+        nc.sync.dma_start(list1[:], offs)
+        nc.scalar.dma_start(
+            out=tab_scale_rows[0:32, :].bitcast(I32), in_=tab_scales.rearrange("a q t -> q a t").bitcast(I32)
+        )
+        nc.vector.memset(tab_scale_rows[32:64, :].bitcast(I32), 0)
+        nc.vector.memset(tab_scale_rows[64:P, :].bitcast(I32), 0)
+        nc.vector.memset(v_scales[:].rearrange("p a c -> p (a c)").bitcast(I32), 0)
+        nc.vector.memset(w4_planes[:].rearrange("p a c -> p (a c)").bitcast(I32), 0)
+        tab = [slot([P, T], I32, "tab%d" % a, "BC"[a]) for a in range(PASSES)]
+        tab_rows = tab_words.rearrange("a p t i -> a p (t i)").bitcast(I32)
+        for a in range(PASSES):
+            nc.sync.dma_start(out=tab[a][:], in_=tab_rows[a])
+        w4_scale_raw = keep.tile([P, PASSES, H], U8, name="w4_scale_raw", align_bytes=64)
+        for quad in range(4):
+            nc.scalar.dma_start(
+                out=w4_scale_raw[32 * quad : 32 * quad + 4, :, :].bitcast(I32),
+                in_=w4_scales[:, 4 * quad : 4 * quad + 4, :].rearrange("a r c -> r a c").bitcast(I32),
+            )
+        w4_raw = slot([P, PASSES, 2 * H], U8, "w4_raw", "E")
+        nc.sync.dma_start(out=w4_raw[:].bitcast(I32), in_=w4_words.rearrange("a p c -> p a c").bitcast(I32))
+        w1_rows = w1.rearrange("(a p i) c -> a p i c", a=PASSES, i=PACK)
+        w1_raw = [slot([P, PACK, H], F32, "w1_raw0", "H")]
+        nc.sync.dma_start(out=w1_raw[0][:], in_=w1_rows[0])
+        nc.sync.dma_start(list2[:], offs2)
+        page_rows = page0.rearrange("(b t q) l -> t b q l", t=PACK, q=8)
+        pages = []
+
+        def load_page(tag):
+            t = len(pages)
+            page = slot([P, T2], F32, "page%d" % t, tag)
+            nc.sync.dma_start(out=page[:], in_=page_rows[t])
+            pages.append(page)
+
+        load_page("I")
+        nc.sync.dma_start(list3[:], offs3)
+
+        picked_scale_rows = keep.tile([P, S], U8, name="picked_scale_rows", align_bytes=64)
+        nc.vector.tensor_copy(picked_scale_rows[:], tab_scale_rows[:].indirect(list1[:]))
+        for quad in range(4):
+            nc.scalar.dma_start(
+                out=v_scales[32 * quad : 32 * quad + 4, :, :].bitcast(I32),
+                in_=picked_scale_rows[8 * quad : 8 * quad + 8, :].bitcast(I32),
+            )
+        v_codes = []
+        for a in range(PASSES):
+            codes = keep.tile([P, S], U32, name="v_codes%d" % a, align_bytes=64)
+            nc.vector.tensor_copy(codes[:], tab[a][:].bitcast(U32).indirect(list1[:]))
+            v_codes.append(codes)
+        w1_raw.append(slot([P, PACK, H], F32, "w1_raw1", "B"))
+        nc.sync.dma_start(out=w1_raw[1][:], in_=w1_rows[1])
+
+        w4_codes = keep.tile([P, PASSES, 2 * H], U8, name="w4_codes", align_bytes=64)
+        nc.vector.tensor_copy(
+            out=w4_codes[:].bitcast(I32).rearrange("p a (t b w) -> p a t b w", t=PACK, w=4),
+            in_=w4_raw[:].bitcast(I32).rearrange("p a (b t w) -> p a t b w", t=PACK, w=4),
+        )
+        for quad in range(4):
+            rows = slice(32 * quad, 32 * quad + 4)
+            nc.vector.tensor_copy(
+                out=w4_planes[rows].bitcast(I32).rearrange("p a (t b w) -> p a t b w", t=PACK, w=2),
+                in_=w4_scale_raw[rows].bitcast(I32).rearrange("p a (b t w) -> p a t b w", t=PACK, w=2),
+            )
+
+        with tc.psum_pool(name="first", bufs=1) as psum:
+            old = []
+            h4 = []
+            first_old = keep.tile([P, S], F32, name="old")
+            nc.vector.tensor_copy(first_old[:], pages[0][:].indirect(list2[:]))
+            old.append(first_old)
+
+            w1_codes = keep.tile([P, PASSES, H], U32, name="w1_codes", align_bytes=64)
+            w1_planes = keep.tile([P, PASSES, H], U8, name="w1_planes", align_bytes=64)
+            for a in range(PASSES):
+                first = slot([P, P, PACK], BF16, "w1_first%d" % a, "FG"[a])
+                nc.vector.tensor_copy(
+                    out=first[:].rearrange("p (b u e) i -> p b u i e", u=2, e=4),
+                    in_=w1_raw[a][:].rearrange("p i (b t u e) -> p t b u i e", t=PACK, u=2, e=4)[:, 0],
+                )
+                nc.vector.quantize_mx(
+                    out=w1_codes[:, a, 0:P].bitcast(FP8X4),
+                    scales=w1_planes[:, a, 0:P],
+                    in_=first[:].rearrange("p m i -> p (m i)"),
+                )
+                rest = slot([P, PACK - 1, P, PACK], BF16, "w1_rest%d" % a, "ED"[a])
+                for t in range(1, PACK):
+                    nc.scalar.copy(
+                        out=rest[:, t - 1].rearrange("p (b u e) i -> p b u i e", u=2, e=4),
+                        in_=w1_raw[a][:].rearrange("p i (b t u e) -> p t b u i e", t=PACK, u=2, e=4)[:, t],
+                    )
+                nc.vector.quantize_mx(
+                    out=w1_codes[:, a, P:H].bitcast(FP8X4),
+                    scales=w1_planes[:, a, P:H],
+                    in_=rest[:].rearrange("p t m i -> p (t m i)"),
+                )
+
+            load_page("H")
+            gains = slot([P, PACK, 8], F32, "gains", "F")
+            gain_rows = gain.rearrange("(b t q o) -> t b q o", t=PACK, q=8, o=1)
+            for t in range(PACK):
+                nc.sync.dma_start(out=gains[:, t, 0:1], in_=gain_rows[t])
+            bias = slot([P, GROUPS, PACK], F32, "bias", "G")
+            nc.sync.dma_start(out=bias[:], in_=b2.rearrange("(g p s) -> p g s", g=GROUPS, s=PACK))
+            w2_rows = w2.rearrange("(b t q) n -> t b q n", t=PACK, q=8)
+            w2_raw = [slot([P, PACK, BANK], F32, "w2_raw%d" % g, "BD"[g]) for g in range(GROUPS)]
+            for g in range(GROUPS):
+                for t in range(PACK):
+                    nc.sync.dma_start(out=w2_raw[g][:, t, :], in_=w2_rows[t][:, :, BANK * g : BANK * (g + 1)])
+
+            w2_codes = keep.tile([P, GROUPS, BANK], U32, name="w2_codes", align_bytes=64)
+            w2_planes = keep.tile([P, GROUPS, BANK], U8, name="w2_planes", align_bytes=64)
+            x_bf = [
+                keep.tile([P, CHUNK, PACK], BF16, name="x_bf%d" % c, align_bytes=64) for c in range(CHUNKS)
+            ]
+
+            for t in range(PACK):
+                for half in range(S // BANK):
+                    cols = slice(half * BANK, (half + 1) * BANK)
+                    acc = psum.tile([P, BANK], F32, name="h4_acc", bufs=2)
+                    for a in range(PASSES):
+                        nc.tensor.matmul_mx(
+                            out=acc[:],
+                            lhsT=w4_codes[:, a, 2 * P * t : 2 * P * (t + 1)].bitcast(FP4X4),
+                            lhsT_scale=w4_planes[:, a, P * t : P * (t + 1)],
+                            rhs=v_codes[a][:, cols].bitcast(FP8X4),
+                            rhs_scale=v_scales[:, a, cols],
+                            start=(a == 0),
+                            stop=(a == PASSES - 1),
+                        )
+                    second = big.tile([P, BANK], F32, name="h4")
+                    nc.scalar.copy(out=second[:], in_=acc[:])
+                    h4.append(second)
+                h = ring.tile([P, S], F32, name="h")
+                for half in range(S // BANK):
+                    cols = slice(half * BANK, (half + 1) * BANK)
+                    acc = psum.tile([P, BANK], F32, name="h1_acc", bufs=4)
+                    for a in range(PASSES):
+                        nc.tensor.matmul_mx(
+                            out=acc[:],
+                            lhsT=w1_codes[:, a, P * t : P * (t + 1)].bitcast(FP8X4),
+                            lhsT_scale=w1_planes[:, a, P * t : P * (t + 1)],
+                            rhs=v_codes[a][:, cols].bitcast(FP8X4),
+                            rhs_scale=v_scales[:, a, cols],
+                            start=(a == 0),
+                            stop=(a == PASSES - 1),
+                        )
+                    nc.vector.tensor_tensor(h[:, cols], acc[:], h4[2 * t + half][:], ALU.max)
+                nc.vector.tensor_tensor(pages[t][:].indirect(list2[:]), old[t][:], h[:], ALU.add)
+                if t + 1 < PACK:
+                    next_old = keep.tile([P, S], F32, name="old")
+                    nc.vector.tensor_copy(next_old[:], pages[t + 1][:].indirect(list2[:]))
+                    old.append(next_old)
+                    read = ring.tile([P, PICKED], F32, name="read")
+                    nc.vector.tensor_copy(read[:], pages[t][:].indirect(list3[:]))
+                    for c in range(CHUNKS):
+                        nc.scalar.activation(
+                            out=x_bf[c][:, :, t],
+                            in_=read[:, c * CHUNK : (c + 1) * CHUNK],
+                            func=ACT.Identity,
+                            scale=gains[:, t, 0:1],
+                        )
+                if t == 0:
+                    for g in range(GROUPS):
+                        rounded = ring.tile([P, PACK, P, PACK], BF16, name="w2_bf", align_bytes=64)
+                        nc.scalar.copy(
+                            out=rounded[:].rearrange("p s m t -> p m t s"),
+                            in_=w2_raw[g][:].rearrange("p t (m s) -> p m t s", s=PACK),
+                        )
+                        nc.vector.quantize_mx(
+                            out=w2_codes[:, g, :].bitcast(FP8X4),
+                            scales=w2_planes[:, g, :],
+                            in_=rounded[:].rearrange("p s m t -> p (s m t)"),
+                        )
+                        load_page("BD"[g])
+
+        last = PACK - 1
+        x_codes = keep.tile([P, PICKED], U32, name="x_codes", align_bytes=64)
+        x_planes = keep.tile([P, PICKED], U8, name="x_planes", align_bytes=64)
+        y_codes = keep.tile([P, GROUPS, PICKED], U32, name="y_codes", align_bytes=64)
+        y_planes = keep.tile([P, GROUPS, PICKED], U8, name="y_planes", align_bytes=64)
+        y_rows = out_0.rearrange("(g p s) j -> p g s j", g=GROUPS, s=PACK)
+        word_rows = out_1.rearrange("g p m t -> p g (m t)").bitcast(I32)
+        with tc.psum_pool(name="second", bufs=8) as psum:
+            for c in range(CHUNKS):
+                cols = slice(c * CHUNK, (c + 1) * CHUNK)
+                read = keep.tile([P, CHUNK], F32, name="read_last%d" % c)
+                nc.vector.tensor_copy(
+                    read[:], pages[last][:].indirect(list3[:, c * CHUNK // 16 : (c + 1) * CHUNK // 16])
+                )
+                nc.scalar.activation(
+                    out=x_bf[c][:, :, last], in_=read[:], func=ACT.Identity, scale=gains[:, last, 0:1]
+                )
+                nc.vector.quantize_mx(
+                    out=x_codes[:, cols].bitcast(FP8X4),
+                    scales=x_planes[:, cols],
+                    in_=x_bf[c][:].rearrange("p j t -> p (j t)"),
+                )
+            for c in range(CHUNKS):
+                cols = slice(c * CHUNK, (c + 1) * CHUNK)
+                y = big.tile([P, GROUPS, PACK, CHUNK], F32, name="y")
+                for g in range(GROUPS):
+                    for pair in range(PACK // 2):
+                        acc = psum.tile([P, 2, CHUNK], F32, name="y_acc")
+                        for e in range(2):
+                            s = 2 * pair + e
+                            nc.tensor.matmul_mx(
+                                out=acc[:, e, :],
+                                lhsT=w2_codes[:, g, P * s : P * (s + 1)].bitcast(FP8X4),
+                                lhsT_scale=w2_planes[:, g, P * s : P * (s + 1)],
+                                rhs=x_codes[:, cols].bitcast(FP8X4),
+                                rhs_scale=x_planes[:, cols],
+                                start=True,
+                                stop=True,
+                            )
+                        for e in range(2):
+                            s = 2 * pair + e
+                            nc.scalar.activation(
+                                out=y[:, g, s, :], in_=acc[:, e, :], func=ACT.Identity, bias=bias[:, g, s : s + 1]
+                            )
+                    nc.sync.dma_start(out=y_rows[:, g, :, cols], in_=y[:, g, :, :])
+                    y_bf = ring.tile([P, CHUNK, PACK], BF16, name="y_bf", align_bytes=64)
+                    nc.vector.tensor_copy(
+                        out=y_bf[:].rearrange("p (u e) s -> p u s e", e=4),
+                        in_=y[:, g, :, :].rearrange("p s (u e) -> p u s e", e=4),
+                    )
+                    nc.vector.quantize_mx(
+                        out=y_codes[:, g, cols].bitcast(FP8X4),
+                        scales=y_planes[:, g, cols],
+                        in_=y_bf[:].rearrange("p j s -> p (j s)"),
+                    )
+                nc.sync.dma_start(out=word_rows[:, :, cols], in_=y_codes[:, :, cols].bitcast(I32))
+            for quad in range(4):
+                nc.sync.dma_start(
+                    out=out_2[:, 4 * quad : 4 * quad + 4, :].rearrange("g r m -> r g m").bitcast(I32),
+                    in_=y_planes[32 * quad : 32 * quad + 4, :, :].bitcast(I32),
+                )

@@ -31,17 +31,16 @@ def tile_list_lift_fault_updates_kernel(
     nc = tc.nc
     with ExitStack() as ctx:
         keep = ctx.enter_context(tc.tile_pool(name="keep", bufs=1))
-        big = ctx.enter_context(tc.tile_pool(name="big", bufs=4))
         ring = ctx.enter_context(tc.tile_pool(name="ring", bufs=2))
 
         list1 = keep.tile([P, S // 16], U16, name="list1")
         list2 = keep.tile([P, S // 16], U16, name="list2")
         list3 = keep.tile([P, PICKED // 16], U16, name="list3")
 
-        def slot(shape, dtype, name, tag):
+        def shared(shape, dtype, name, tag):
             return keep.tile(shape, dtype, name=name, tag=tag, align_bytes=64)
 
-        tab_scale_rows = slot([P, T], U8, "tab_scale_rows", "A")
+        tab_scale_rows = keep.tile([P, T], U8, name="tab_scale_rows", align_bytes=64)
         v_scales = keep.tile([P, PASSES, S], U8, name="v_scales", align_bytes=64)
         w4_planes = keep.tile([P, PASSES, H], U8, name="w4_planes", align_bytes=64)
 
@@ -53,7 +52,7 @@ def tile_list_lift_fault_updates_kernel(
         nc.vector.memset(tab_scale_rows[64:P, :].bitcast(I32), 0)
         nc.vector.memset(v_scales[:].rearrange("p a c -> p (a c)").bitcast(I32), 0)
         nc.vector.memset(w4_planes[:].rearrange("p a c -> p (a c)").bitcast(I32), 0)
-        tab = [slot([P, T], I32, "tab%d" % a, "BC"[a]) for a in range(PASSES)]
+        tab = [shared([P, T], I32, "tab%d" % a, "tab_then_y%d" % a) for a in range(PASSES)]
         tab_rows = tab_words.rearrange("a p t i -> a p (t i)").bitcast(I32)
         for a in range(PASSES):
             nc.sync.dma_start(out=tab[a][:], in_=tab_rows[a])
@@ -63,23 +62,36 @@ def tile_list_lift_fault_updates_kernel(
                 out=w4_scale_raw[32 * quad : 32 * quad + 4, :, :].bitcast(I32),
                 in_=w4_scales[:, 4 * quad : 4 * quad + 4, :].rearrange("a r c -> r a c").bitcast(I32),
             )
-        w4_raw = slot([P, PASSES, 2 * H], U8, "w4_raw", "E")
+        w4_raw = keep.tile([P, PASSES, 2 * H], U8, name="w4_raw", align_bytes=64)
         nc.sync.dma_start(out=w4_raw[:].bitcast(I32), in_=w4_words.rearrange("a p c -> p a c").bitcast(I32))
         w1_rows = w1.rearrange("(a p i) c -> a p i c", a=PASSES, i=PACK)
-        w1_raw = [slot([P, PACK, H], F32, "w1_raw0", "H")]
+        w1_raw = [shared([P, PACK, H], F32, "w1_raw0", "w1_then_y0")]
         nc.sync.dma_start(out=w1_raw[0][:], in_=w1_rows[0])
         nc.sync.dma_start(list2[:], offs2)
         page_rows = page0.rearrange("(b t q) l -> t b q l", t=PACK, q=8)
-        pages = []
+        pages = [keep.tile([P, T2], F32, name="page%d" % t) for t in range(PACK)]
 
-        def load_page(tag):
-            t = len(pages)
-            page = slot([P, T2], F32, "page%d" % t, tag)
-            nc.sync.dma_start(out=page[:], in_=page_rows[t])
-            pages.append(page)
+        def load_page(t):
+            nc.sync.dma_start(out=pages[t][:], in_=page_rows[t])
 
-        load_page("I")
+        load_page(0)
+        w1_raw.append(shared([P, PACK, H], F32, "w1_raw1", "w1_then_y1"))
+        nc.sync.dma_start(out=w1_raw[1][:], in_=w1_rows[1])
         nc.sync.dma_start(list3[:], offs3)
+        w2_rows = w2.rearrange("(b t q) n -> t b q n", t=PACK, q=8)
+        w2_raw = [shared([P, PACK, BANK], F32, "w2_raw%d" % g, "w2_raw_then_x%d" % g) for g in range(GROUPS)]
+        for g in range(GROUPS):
+            for t in range(PACK):
+                nc.sync.dma_start(out=w2_raw[g][:, t, :], in_=w2_rows[t][:, :, BANK * g : BANK * (g + 1)])
+        load_page(1)
+        gains = keep.tile([P, PACK, 8], F32, name="gains")
+        gain_rows = gain.rearrange("(b t q o) -> t b q o", t=PACK, q=8, o=1)
+        for t in range(PACK):
+            nc.sync.dma_start(out=gains[:, t, 0:1], in_=gain_rows[t])
+        bias = keep.tile([P, GROUPS, PACK], F32, name="bias")
+        nc.sync.dma_start(out=bias[:], in_=b2.rearrange("(g p s) -> p g s", g=GROUPS, s=PACK))
+        load_page(2)
+        load_page(3)
 
         picked_scale_rows = keep.tile([P, S], U8, name="picked_scale_rows", align_bytes=64)
         nc.vector.tensor_copy(picked_scale_rows[:], tab_scale_rows[:].indirect(list1[:]))
@@ -93,8 +105,6 @@ def tile_list_lift_fault_updates_kernel(
             codes = keep.tile([P, S], U32, name="v_codes%d" % a, align_bytes=64)
             nc.vector.tensor_copy(codes[:], tab[a][:].bitcast(U32).indirect(list1[:]))
             v_codes.append(codes)
-        w1_raw.append(slot([P, PACK, H], F32, "w1_raw1", "B"))
-        nc.sync.dma_start(out=w1_raw[1][:], in_=w1_rows[1])
 
         w4_codes = keep.tile([P, PASSES, 2 * H], U8, name="w4_codes", align_bytes=64)
         nc.vector.tensor_copy(
@@ -111,14 +121,14 @@ def tile_list_lift_fault_updates_kernel(
         with tc.psum_pool(name="first", bufs=1) as psum:
             old = []
             h4 = []
-            first_old = keep.tile([P, S], F32, name="old")
+            first_old = ring.tile([P, S], F32, name="old")
             nc.vector.tensor_copy(first_old[:], pages[0][:].indirect(list2[:]))
             old.append(first_old)
 
             w1_codes = keep.tile([P, PASSES, H], U32, name="w1_codes", align_bytes=64)
             w1_planes = keep.tile([P, PASSES, H], U8, name="w1_planes", align_bytes=64)
             for a in range(PASSES):
-                first = slot([P, P, PACK], BF16, "w1_first%d" % a, "FG"[a])
+                first = keep.tile([P, P, PACK], BF16, name="w1_first%d" % a, align_bytes=64)
                 nc.vector.tensor_copy(
                     out=first[:].rearrange("p (b u e) i -> p b u i e", u=2, e=4),
                     in_=w1_raw[a][:].rearrange("p i (b t u e) -> p t b u i e", t=PACK, u=2, e=4)[:, 0],
@@ -128,7 +138,7 @@ def tile_list_lift_fault_updates_kernel(
                     scales=w1_planes[:, a, 0:P],
                     in_=first[:].rearrange("p m i -> p (m i)"),
                 )
-                rest = slot([P, PACK - 1, P, PACK], BF16, "w1_rest%d" % a, "ED"[a])
+                rest = keep.tile([P, PACK - 1, P, PACK], BF16, name="w1_rest%d" % a, align_bytes=64)
                 for t in range(1, PACK):
                     nc.scalar.copy(
                         out=rest[:, t - 1].rearrange("p (b u e) i -> p b u i e", u=2, e=4),
@@ -140,24 +150,23 @@ def tile_list_lift_fault_updates_kernel(
                     in_=rest[:].rearrange("p t m i -> p (t m i)"),
                 )
 
-            load_page("H")
-            gains = slot([P, PACK, 8], F32, "gains", "F")
-            gain_rows = gain.rearrange("(b t q o) -> t b q o", t=PACK, q=8, o=1)
-            for t in range(PACK):
-                nc.sync.dma_start(out=gains[:, t, 0:1], in_=gain_rows[t])
-            bias = slot([P, GROUPS, PACK], F32, "bias", "G")
-            nc.sync.dma_start(out=bias[:], in_=b2.rearrange("(g p s) -> p g s", g=GROUPS, s=PACK))
-            w2_rows = w2.rearrange("(b t q) n -> t b q n", t=PACK, q=8)
-            w2_raw = [slot([P, PACK, BANK], F32, "w2_raw%d" % g, "BD"[g]) for g in range(GROUPS)]
-            for g in range(GROUPS):
-                for t in range(PACK):
-                    nc.sync.dma_start(out=w2_raw[g][:, t, :], in_=w2_rows[t][:, :, BANK * g : BANK * (g + 1)])
-
             w2_codes = keep.tile([P, GROUPS, BANK], U32, name="w2_codes", align_bytes=64)
             w2_planes = keep.tile([P, GROUPS, BANK], U8, name="w2_planes", align_bytes=64)
-            x_bf = [
-                keep.tile([P, CHUNK, PACK], BF16, name="x_bf%d" % c, align_bytes=64) for c in range(CHUNKS)
-            ]
+            def quantise_w2():
+                for g in range(GROUPS):
+                    rounded = shared([P, PACK, P, PACK], BF16, "w2_bf%d" % g, "w2_bf_then_x%d" % g)
+                    nc.scalar.copy(
+                        out=rounded[:].rearrange("p s m t -> p m t s"),
+                        in_=w2_raw[g][:].rearrange("p t (m s) -> p m t s", s=PACK),
+                    )
+                    nc.vector.quantize_mx(
+                        out=w2_codes[:, g, :].bitcast(FP8X4),
+                        scales=w2_planes[:, g, :],
+                        in_=rounded[:].rearrange("p s m t -> p (s m t)"),
+                    )
+
+            x_bf = []
+            x_tags = ["w2_raw_then_x0", "w2_raw_then_x1", "w2_bf_then_x0", "w2_bf_then_x1"]
 
             for t in range(PACK):
                 for half in range(S // BANK):
@@ -173,13 +182,13 @@ def tile_list_lift_fault_updates_kernel(
                             start=(a == 0),
                             stop=(a == PASSES - 1),
                         )
-                    second = big.tile([P, BANK], F32, name="h4")
+                    second = keep.tile([P, BANK], F32, name="h4", bufs=8)
                     nc.scalar.copy(out=second[:], in_=acc[:])
                     h4.append(second)
                 h = ring.tile([P, S], F32, name="h")
                 for half in range(S // BANK):
                     cols = slice(half * BANK, (half + 1) * BANK)
-                    acc = psum.tile([P, BANK], F32, name="h1_acc", bufs=4)
+                    acc = psum.tile([P, BANK], F32, name="h1_acc", bufs=6)
                     for a in range(PASSES):
                         nc.tensor.matmul_mx(
                             out=acc[:],
@@ -193,9 +202,12 @@ def tile_list_lift_fault_updates_kernel(
                     nc.vector.tensor_tensor(h[:, cols], acc[:], h4[2 * t + half][:], ALU.max)
                 nc.vector.tensor_tensor(pages[t][:].indirect(list2[:]), old[t][:], h[:], ALU.add)
                 if t + 1 < PACK:
-                    next_old = keep.tile([P, S], F32, name="old")
+                    next_old = ring.tile([P, S], F32, name="old")
                     nc.vector.tensor_copy(next_old[:], pages[t + 1][:].indirect(list2[:]))
                     old.append(next_old)
+                    if t == 0:
+                        quantise_w2()
+                        x_bf.extend(shared([P, CHUNK, PACK], BF16, "x_bf%d" % c, x_tags[c]) for c in range(CHUNKS))
                     read = ring.tile([P, PICKED], F32, name="read")
                     nc.vector.tensor_copy(read[:], pages[t][:].indirect(list3[:]))
                     for c in range(CHUNKS):
@@ -205,21 +217,9 @@ def tile_list_lift_fault_updates_kernel(
                             func=ACT.Identity,
                             scale=gains[:, t, 0:1],
                         )
-                if t == 0:
-                    for g in range(GROUPS):
-                        rounded = ring.tile([P, PACK, P, PACK], BF16, name="w2_bf", align_bytes=64)
-                        nc.scalar.copy(
-                            out=rounded[:].rearrange("p s m t -> p m t s"),
-                            in_=w2_raw[g][:].rearrange("p t (m s) -> p m t s", s=PACK),
-                        )
-                        nc.vector.quantize_mx(
-                            out=w2_codes[:, g, :].bitcast(FP8X4),
-                            scales=w2_planes[:, g, :],
-                            in_=rounded[:].rearrange("p s m t -> p (s m t)"),
-                        )
-                        load_page("BD"[g])
 
         last = PACK - 1
+        y_tags = ["tab_then_y0", "tab_then_y1", "w1_then_y0", "w1_then_y1"]
         x_codes = keep.tile([P, PICKED], U32, name="x_codes", align_bytes=64)
         x_planes = keep.tile([P, PICKED], U8, name="x_planes", align_bytes=64)
         y_codes = keep.tile([P, GROUPS, PICKED], U32, name="y_codes", align_bytes=64)
@@ -243,7 +243,7 @@ def tile_list_lift_fault_updates_kernel(
                 )
             for c in range(CHUNKS):
                 cols = slice(c * CHUNK, (c + 1) * CHUNK)
-                y = big.tile([P, GROUPS, PACK, CHUNK], F32, name="y")
+                y = shared([P, GROUPS, PACK, CHUNK], F32, "y%d" % c, y_tags[c])
                 for g in range(GROUPS):
                     for pair in range(PACK // 2):
                         acc = psum.tile([P, 2, CHUNK], F32, name="y_acc")
@@ -276,7 +276,8 @@ def tile_list_lift_fault_updates_kernel(
                     )
                 nc.sync.dma_start(out=word_rows[:, :, cols], in_=y_codes[:, :, cols].bitcast(I32))
             for quad in range(4):
-                nc.sync.dma_start(
+                queue = nc.scalar if quad % 2 else nc.sync
+                queue.dma_start(
                     out=out_2[:, 4 * quad : 4 * quad + 4, :].rearrange("g r m -> r g m").bitcast(I32),
                     in_=y_planes[32 * quad : 32 * quad + 4, :, :].bitcast(I32),
                 )

from contextlib import ExitStack

import concourse.mybir as mybir

K, T, S, H, T2, PICKED, N = 1024, 2048, 1024, 512, 2048, 1024, 1024
FLOPS = 2 * (2 * K * H * S + H * N * PICKED)

F32 = mybir.dt.float32
BF16 = mybir.dt.bfloat16
I32 = mybir.dt.int32
U32 = mybir.dt.uint32
U16 = mybir.dt.uint16
U8 = mybir.dt.uint8
FP8X4 = mybir.dt.float8_e4m3fn_x4
FP4X4 = mybir.dt.float4_e2m1fn_x4
ALU = mybir.AluOpType
ACT = mybir.ActivationFunctionType

P = 128
PACK = 4
PASSES = K // (P * PACK)
GROUPS = N // (P * PACK)
BANK = 512
CHUNK = 256
CHUNKS = PICKED // CHUNK


def tile_list_lift_fault_updates_kernel(
    tc, tab_words, tab_scales, offs, offs2, offs3, w1, w4_words, w4_scales, page0, gain, w2, b2, out_0, out_1, out_2
):
    nc = tc.nc
    with ExitStack() as ctx:
        keep = ctx.enter_context(tc.tile_pool(name="keep", bufs=1))
        ring = ctx.enter_context(tc.tile_pool(name="ring", bufs=2))

        list1 = keep.tile([P, S // 16], U16, name="list1")
        list2 = keep.tile([P, S // 16], U16, name="list2")
        list3 = keep.tile([P, PICKED // 16], U16, name="list3")

        def shared(shape, dtype, name, tag):
            return keep.tile(shape, dtype, name=name, tag=tag, align_bytes=64)

        tab_scale_rows = keep.tile([P, T], U8, name="tab_scale_rows", align_bytes=64)
        v_scales = keep.tile([P, PASSES, S], U8, name="v_scales", align_bytes=64)
        w4_planes = keep.tile([P, PASSES, H], U8, name="w4_planes", align_bytes=64)

        nc.sync.dma_start(list1[:], offs)
        nc.scalar.dma_start(
            out=tab_scale_rows[0:32, :].bitcast(I32), in_=tab_scales.rearrange("a q t -> q a t").bitcast(I32)
        )
        nc.vector.memset(tab_scale_rows[32:64, :].bitcast(I32), 0)
        nc.vector.memset(tab_scale_rows[64:P, :].bitcast(I32), 0)
        nc.vector.memset(v_scales[:].rearrange("p a c -> p (a c)").bitcast(I32), 0)
        nc.vector.memset(w4_planes[:].rearrange("p a c -> p (a c)").bitcast(I32), 0)
        tab = [shared([P, T], I32, "tab%d" % a, "tab_then_y%d" % a) for a in range(PASSES)]
        tab_rows = tab_words.rearrange("a p t i -> a p (t i)").bitcast(I32)
        for a in range(PASSES):
            nc.sync.dma_start(out=tab[a][:], in_=tab_rows[a])
        w4_scale_raw = keep.tile([P, PASSES, H], U8, name="w4_scale_raw", align_bytes=64)
        for quad in range(4):
            nc.scalar.dma_start(
                out=w4_scale_raw[32 * quad : 32 * quad + 4, :, :].bitcast(I32),
                in_=w4_scales[:, 4 * quad : 4 * quad + 4, :].rearrange("a r c -> r a c").bitcast(I32),
            )
        w4_raw = keep.tile([P, PASSES, 2 * H], U8, name="w4_raw", align_bytes=64)
        nc.sync.dma_start(out=w4_raw[:].bitcast(I32), in_=w4_words.rearrange("a p c -> p a c").bitcast(I32))
        w1_rows = w1.rearrange("(a p i) c -> a p i c", a=PASSES, i=PACK)
        w1_raw = [shared([P, PACK, H], F32, "w1_raw0", "w1_then_y0")]
        nc.sync.dma_start(out=w1_raw[0][:], in_=w1_rows[0])
        nc.sync.dma_start(list2[:], offs2)
        page_rows = page0.rearrange("(b t q) l -> t b q l", t=PACK, q=8)
        pages = [keep.tile([P, T2], F32, name="page%d" % t) for t in range(PACK)]

        def load_page(t):
            nc.sync.dma_start(out=pages[t][:], in_=page_rows[t])

        load_page(0)
        w1_raw.append(shared([P, PACK, H], F32, "w1_raw1", "w1_then_y1"))
        nc.sync.dma_start(out=w1_raw[1][:], in_=w1_rows[1])
        nc.sync.dma_start(list3[:], offs3)
        w2_rows = w2.rearrange("(b t q) n -> t b q n", t=PACK, q=8)
        w2_raw = [shared([P, PACK, BANK], F32, "w2_raw%d" % g, "w2_raw_then_x%d" % g) for g in range(GROUPS)]
        for g in range(GROUPS):
            for t in range(PACK):
                nc.sync.dma_start(out=w2_raw[g][:, t, :], in_=w2_rows[t][:, :, BANK * g : BANK * (g + 1)])
        load_page(1)
        gains = keep.tile([P, PACK, 8], F32, name="gains")
        gain_rows = gain.rearrange("(b t q o) -> t b q o", t=PACK, q=8, o=1)
        for t in range(PACK):
            nc.sync.dma_start(out=gains[:, t, 0:1], in_=gain_rows[t])
        bias = keep.tile([P, GROUPS, PACK], F32, name="bias")
        nc.sync.dma_start(out=bias[:], in_=b2.rearrange("(g p s) -> p g s", g=GROUPS, s=PACK))
        load_page(2)
        load_page(3)

        picked_scale_rows = keep.tile([P, S], U8, name="picked_scale_rows", align_bytes=64)
        nc.vector.tensor_copy(picked_scale_rows[:], tab_scale_rows[:].indirect(list1[:]))
        for quad in range(4):
            nc.scalar.dma_start(
                out=v_scales[32 * quad : 32 * quad + 4, :, :].bitcast(I32),
                in_=picked_scale_rows[8 * quad : 8 * quad + 8, :].bitcast(I32),
            )
        v_codes = []
        for a in range(PASSES):
            codes = keep.tile([P, S], U32, name="v_codes%d" % a, align_bytes=64)
            nc.vector.tensor_copy(codes[:], tab[a][:].bitcast(U32).indirect(list1[:]))
            v_codes.append(codes)

        w4_codes = keep.tile([P, PASSES, 2 * H], U8, name="w4_codes", align_bytes=64)
        nc.vector.tensor_copy(
            out=w4_codes[:].bitcast(I32).rearrange("p a (t b w) -> p a t b w", t=PACK, w=4),
            in_=w4_raw[:].bitcast(I32).rearrange("p a (b t w) -> p a t b w", t=PACK, w=4),
        )
        for quad in range(4):
            rows = slice(32 * quad, 32 * quad + 4)
            nc.vector.tensor_copy(
                out=w4_planes[rows].bitcast(I32).rearrange("p a (t b w) -> p a t b w", t=PACK, w=2),
                in_=w4_scale_raw[rows].bitcast(I32).rearrange("p a (b t w) -> p a t b w", t=PACK, w=2),
            )

        with tc.psum_pool(name="first", bufs=1) as psum:
            old = []
            h4 = []
            first_old = ring.tile([P, S], F32, name="old")
            nc.vector.tensor_copy(first_old[:], pages[0][:].indirect(list2[:]))
            old.append(first_old)

            w1_codes = keep.tile([P, PASSES, H], U32, name="w1_codes", align_bytes=64)
            w1_planes = keep.tile([P, PASSES, H], U8, name="w1_planes", align_bytes=64)
            for a in range(PASSES):
                first = keep.tile([P, P, PACK], BF16, name="w1_first%d" % a, align_bytes=64)
                nc.vector.tensor_copy(
                    out=first[:].rearrange("p (b u e) i -> p b u i e", u=2, e=4),
                    in_=w1_raw[a][:].rearrange("p i (b t u e) -> p t b u i e", t=PACK, u=2, e=4)[:, 0],
                )
                nc.vector.quantize_mx(
                    out=w1_codes[:, a, 0:P].bitcast(FP8X4),
                    scales=w1_planes[:, a, 0:P],
                    in_=first[:].rearrange("p m i -> p (m i)"),
                )
                rest = keep.tile([P, PACK - 1, P, PACK], BF16, name="w1_rest%d" % a, align_bytes=64)
                for t in range(1, PACK):
                    nc.scalar.copy(
                        out=rest[:, t - 1].rearrange("p (b u e) i -> p b u i e", u=2, e=4),
                        in_=w1_raw[a][:].rearrange("p i (b t u e) -> p t b u i e", t=PACK, u=2, e=4)[:, t],
                    )
                nc.vector.quantize_mx(
                    out=w1_codes[:, a, P:H].bitcast(FP8X4),
                    scales=w1_planes[:, a, P:H],
                    in_=rest[:].rearrange("p t m i -> p (t m i)"),
                )

            w2_codes = keep.tile([P, GROUPS, BANK], U32, name="w2_codes", align_bytes=64)
            w2_planes = keep.tile([P, GROUPS, BANK], U8, name="w2_planes", align_bytes=64)
            def quantise_w2():
                for g in range(GROUPS):
                    rounded = shared([P, PACK, P, PACK], BF16, "w2_bf%d" % g, "w2_bf_then_x%d" % g)
                    nc.scalar.copy(
                        out=rounded[:].rearrange("p s m t -> p m t s"),
                        in_=w2_raw[g][:].rearrange("p t (m s) -> p m t s", s=PACK),
                    )
                    nc.vector.quantize_mx(
                        out=w2_codes[:, g, :].bitcast(FP8X4),
                        scales=w2_planes[:, g, :],
                        in_=rounded[:].rearrange("p s m t -> p (s m t)"),
                    )

            x_bf = []
            x_tags = ["w2_raw_then_x0", "w2_raw_then_x1", "w2_bf_then_x0", "w2_bf_then_x1"]

            for t in range(PACK):
                for half in range(S // BANK):
                    cols = slice(half * BANK, (half + 1) * BANK)
                    acc = psum.tile([P, BANK], F32, name="h4_acc", bufs=2)
                    for a in range(PASSES):
                        nc.tensor.matmul_mx(
                            out=acc[:],
                            lhsT=w4_codes[:, a, 2 * P * t : 2 * P * (t + 1)].bitcast(FP4X4),
                            lhsT_scale=w4_planes[:, a, P * t : P * (t + 1)],
                            rhs=v_codes[a][:, cols].bitcast(FP8X4),
                            rhs_scale=v_scales[:, a, cols],
                            start=(a == 0),
                            stop=(a == PASSES - 1),
                        )
                    second = keep.tile([P, BANK], F32, name="h4", bufs=8)
                    nc.scalar.copy(out=second[:], in_=acc[:])
                    h4.append(second)
                h = ring.tile([P, S], F32, name="h")
                for half in range(S // BANK):
                    cols = slice(half * BANK, (half + 1) * BANK)
                    acc = psum.tile([P, BANK], F32, name="h1_acc", bufs=6)
                    for a in range(PASSES):
                        nc.tensor.matmul_mx(
                            out=acc[:],
                            lhsT=w1_codes[:, a, P * t : P * (t + 1)].bitcast(FP8X4),
                            lhsT_scale=w1_planes[:, a, P * t : P * (t + 1)],
                            rhs=v_codes[a][:, cols].bitcast(FP8X4),
                            rhs_scale=v_scales[:, a, cols],
                            start=(a == 0),
                            stop=(a == PASSES - 1),
                        )
                    nc.vector.tensor_tensor(h[:, cols], acc[:], h4[2 * t + half][:], ALU.max)
                nc.vector.tensor_tensor(pages[t][:].indirect(list2[:]), old[t][:], h[:], ALU.add)
                if t + 1 < PACK:
                    next_old = ring.tile([P, S], F32, name="old")
                    nc.vector.tensor_copy(next_old[:], pages[t + 1][:].indirect(list2[:]))
                    old.append(next_old)
                    if t == 0:
                        quantise_w2()
                        x_bf.extend(shared([P, CHUNK, PACK], BF16, "x_bf%d" % c, x_tags[c]) for c in range(CHUNKS))
                    read = ring.tile([P, PICKED], F32, name="read")
                    nc.vector.tensor_copy(read[:], pages[t][:].indirect(list3[:]))
                    for c in range(CHUNKS):
                        nc.scalar.activation(
                            out=x_bf[c][:, :, t],
                            in_=read[:, c * CHUNK : (c + 1) * CHUNK],
                            func=ACT.Identity,
                            scale=gains[:, t, 0:1],
                        )

        last = PACK - 1
        y_tags = ["tab_then_y0", "tab_then_y1", "w1_then_y0", "w1_then_y1"]
        x_codes = keep.tile([P, PICKED], U32, name="x_codes", align_bytes=64)
        x_planes = keep.tile([P, PICKED], U8, name="x_planes", align_bytes=64)
        y_codes = keep.tile([P, GROUPS, PICKED], U32, name="y_codes", align_bytes=64)
        y_planes = keep.tile([P, GROUPS, PICKED], U8, name="y_planes", align_bytes=64)
        y_rows = out_0.rearrange("(g p s) j -> p g s j", g=GROUPS, s=PACK)
        word_rows = out_1.rearrange("g p m t -> p g (m t)").bitcast(I32)
        with tc.psum_pool(name="second", bufs=8) as psum:
            for c in range(CHUNKS):
                cols = slice(c * CHUNK, (c + 1) * CHUNK)
                read = keep.tile([P, CHUNK], F32, name="read_last%d" % c)
                nc.vector.tensor_copy(
                    read[:], pages[last][:].indirect(list3[:, c * CHUNK // 16 : (c + 1) * CHUNK // 16])
                )
                nc.scalar.activation(
                    out=x_bf[c][:, :, last], in_=read[:], func=ACT.Identity, scale=gains[:, last, 0:1]
                )
                nc.vector.quantize_mx(
                    out=x_codes[:, cols].bitcast(FP8X4),
                    scales=x_planes[:, cols],
                    in_=x_bf[c][:].rearrange("p j t -> p (j t)"),
                )
            for c in range(CHUNKS):
                cols = slice(c * CHUNK, (c + 1) * CHUNK)
                y = shared([P, GROUPS, PACK, CHUNK], F32, "y%d" % c, y_tags[c])
                for g in range(GROUPS):
                    for pair in range(PACK // 2):
                        acc = psum.tile([P, 2, CHUNK], F32, name="y_acc")
                        for e in range(2):
                            s = 2 * pair + e
                            nc.tensor.matmul_mx(
                                out=acc[:, e, :],
                                lhsT=w2_codes[:, g, P * s : P * (s + 1)].bitcast(FP8X4),
                                lhsT_scale=w2_planes[:, g, P * s : P * (s + 1)],
                                rhs=x_codes[:, cols].bitcast(FP8X4),
                                rhs_scale=x_planes[:, cols],
                                start=True,
                                stop=True,
                            )
                        for e in range(2):
                            s = 2 * pair + e
                            nc.scalar.activation(
                                out=y[:, g, s, :], in_=acc[:, e, :], func=ACT.Identity, bias=bias[:, g, s : s + 1]
                            )
                    nc.sync.dma_start(out=y_rows[:, g, :, cols], in_=y[:, g, :, :])
                    y_bf = ring.tile([P, CHUNK, PACK], BF16, name="y_bf", align_bytes=64)
                    nc.vector.tensor_copy(
                        out=y_bf[:].rearrange("p (u e) s -> p u s e", e=4),
                        in_=y[:, g, :, :].rearrange("p s (u e) -> p u s e", e=4),
                    )
                    nc.vector.quantize_mx(
                        out=y_codes[:, g, cols].bitcast(FP8X4),
                        scales=y_planes[:, g, cols],
                        in_=y_bf[:].rearrange("p j s -> p (j s)"),
                    )
                nc.sync.dma_start(out=word_rows[:, :, cols], in_=y_codes[:, :, cols].bitcast(I32))
            for quad in range(4):
                queue = nc.scalar if quad % 2 else nc.sync
                queue.dma_start(
                    out=out_2[:, 4 * quad : 4 * quad + 4, :].rearrange("g r m -> r g m").bitcast(I32),
                    in_=y_planes[32 * quad : 32 * quad + 4, :, :].bitcast(I32),
                )
